import numpy as np
import ml_dtypes


def mxq(x, axis, fmt="e4m3"):
    dtype, down = {"e4m3": (ml_dtypes.float8_e4m3fn, 7), "e5m2": (ml_dtypes.float8_e5m2, 14)}[fmt]
    v = np.moveaxis(np.asarray(x, np.float32).astype(ml_dtypes.bfloat16).astype(np.float64), axis, -1)
    blocks = v.reshape(v.shape[:-1] + (-1, 32))
    amax = np.abs(blocks).max(-1, keepdims=True)
    byte = np.maximum(np.where(amax > 0, np.frexp(amax)[1] - 1 + 127, 0) - down, 1)
    scale = np.exp2(byte - 127.0)
    codes = (blocks / scale).astype(np.float32).astype(dtype).astype(np.float64)
    return np.moveaxis((codes * scale).reshape(v.shape), -1, axis)


WIDE = False


def mx_kscale(k):
    if not WIDE:
        return np.ones(k)
    levels = np.array([10, -10, 5, -5, 0])
    if k % 512:
        return np.exp2(np.random.permutation(np.resize(levels, k // 32))).repeat(32)
    a = np.empty((k // 512, 16))
    for p in range(k // 512):
        a[p, :8] = np.random.permutation(np.resize(levels, 8))
        for g in range(8):
            far = levels[np.abs(levels - a[p, g]) >= 10]
            a[p, g + 8] = far[np.random.randint(len(far))]
    return np.exp2(a.ravel()).repeat(32)


def f64(x):
    return np.asarray(x).astype(np.float64)


def striped(idx):
    return np.tile(idx.reshape(-1, 16).T, (8, 1)).astype(np.uint16)


def unstriped(offs):
    return offs[:16].T.reshape(-1).astype(np.int64)


def pack_weight(w):
    k, n = w.shape
    w = f64(np.asarray(w, np.float32).astype(ml_dtypes.bfloat16)).reshape(k // 32, 32, n)
    amax = np.abs(w).max(1)
    byte = np.clip(np.where(amax > 0, np.frexp(amax)[1] - 1 + 127 - 7, 1), 1, 254)
    scaled = (w * np.exp2(127.0 - byte)[:, None, :]).reshape(k, n).astype(np.float32)
    words = np.ascontiguousarray(scaled.reshape(k // 512, 128, 4, n).transpose(0, 1, 3, 2)).astype(ml_dtypes.float8_e4m3fn).view(np.uint8)
    return words, np.ascontiguousarray(byte.astype(np.uint8).reshape(k // 512, 16, n))


def unpack_weight(words, scales):
    g, p, n, _ = words.shape
    vals = np.ascontiguousarray(words).view(ml_dtypes.float8_e4m3fn).astype(np.float64) * np.repeat(np.exp2(scales.astype(np.float64) - 127.0), 8, axis=1)[..., None]
    return vals.transpose(0, 1, 3, 2).reshape(g * 512, n)


def relu(v):
    return np.maximum(v, 0.0)


def sigmoid(v):
    return 1.0 / (1.0 + np.exp(-np.maximum(v, -700.0)))


K, T, S, D, N = 1024, 1024, 512, 8, 128


def setup_inputs():
    n = np.random.standard_normal
    s = mx_kscale(K)[:, None]
    packed_xT = pack_weight(n((K, T)) * s)
    return {
        "x_words": packed_xT[0],
        "x_scales": packed_xT[1],
        "w1": (n((K, N)) / np.sqrt(K) / s).astype(np.float32),
        "lm": (np.random.uniform(0.3, 1.0, (N, 1))).astype(np.float32),
        "sc": (np.random.uniform(0.4, 0.8, (N, 1))).astype(np.float32),
        "offs": striped(np.random.permutation(T)[:S]),
    }


def reference(x_words, x_scales, w1, lm, sc, offs):
    xq = unpack_weight(x_words, x_scales)[:, unstriped(offs)]
    y = mxq(f64(w1), 0, "e4m3").T @ xq
    bl = y + f64(lm)
    gg = f64(sc) * ((relu(bl)) ** 2)
    mg = gg.reshape(len(gg), -1, D).max(axis=2)
    pk = np.repeat(mg, D, axis=1)
    on = (sigmoid(8.0 * (gg - pk + 0.1))) * (sigmoid(4.0 * (gg - 0.5)))
    return on * (f64(sc) * bl)

@@ -1,0 +1,151 @@
+from contextlib import ExitStack
+
+import concourse.mybir as mybir
+
+K, T, S, D, M = 1024, 1024, 512, 8, 128
+FLOPS = 2 * K * M * S
+
+F32 = mybir.dt.float32
+BF16 = mybir.dt.bfloat16
+I32 = mybir.dt.int32
+U32 = mybir.dt.uint32
+U16 = mybir.dt.uint16
+U8 = mybir.dt.uint8
+FP8X4 = mybir.dt.float8_e4m3fn_x4
+ACT = mybir.ActivationFunctionType
+ALU = mybir.AluOpType
+AX = mybir.AxisListType
+
+P = 128
+PACK = 4
+PASSES = K // (P * PACK)
+
+
+def tile_picked_yspike_amp_p_kernel(tc, x_words, x_scales, w1, lm, sc, offs, out):
+    nc = tc.nc
+    with ExitStack() as ctx:
+        keep = ctx.enter_context(tc.tile_pool(name="keep", bufs=1))
+        psum = ctx.enter_context(tc.psum_pool(name="psum", bufs=1))
+
+        offsets = keep.tile([P, S // 16], U16, name="offsets")
+        nc.sync.dma_start(offsets[:], offs)
+
+        scale_table = keep.tile([P, T], U8, name="scale_table", align_bytes=64)
+        nc.vector.memset(scale_table[:].bitcast(I32), 0)
+
+        lm_col = keep.tile([P, 1], F32, name="lm_col")
+        sc_col = keep.tile([P, 1], F32, name="sc_col")
+        nc.gpsimd.dma_start(out=sc_col[:], in_=sc)
+        nc.gpsimd.dma_start(out=lm_col[:], in_=lm)
+
+        word_table = [keep.tile([P, T], U32, name=f"word_table{g}", align_bytes=64) for g in range(PASSES)]
+        w_raw = [keep.tile([P, PACK, M], F32, name=f"w_raw{g}") for g in range(PASSES)]
+
+        def load_words(g):
+            nc.sync.dma_start(
+                out=word_table[g][:].bitcast(I32),
+                in_=x_words[g].rearrange("p n t -> p (n t)").bitcast(I32),
+            )
+
+        load_words(0)
+        scale_rows = x_scales.bitcast(I32)
+        for q in range(4):
+            nc.sync.dma_start(
+                out=scale_table[32 * q : 32 * q + 4 * PASSES, :].bitcast(I32),
+                in_=scale_rows[:, 4 * q : 4 * q + 4, :],
+            )
+        for g in range(PASSES):
+            nc.sync.dma_start(out=w_raw[g][:], in_=w1[512 * g : 512 * (g + 1), :].rearrange("(p j) m -> p j m", j=PACK))
+        load_words(1)
+
+        quarter_sc = keep.tile([P, 1], F32, name="quarter_sc")
+        quarter_sc_lm = keep.tile([P, 1], F32, name="quarter_sc_lm")
+        nc.scalar.activation(out=quarter_sc[:], in_=sc_col[:], func=ACT.Copy, scale=0.25)
+        nc.gpsimd.tensor_tensor(quarter_sc_lm[:], quarter_sc[:], lm_col[:], ALU.mult)
+
+        w_bf = keep.tile([P, PASSES, M, PACK], BF16, name="w_bf", align_bytes=64)
+        for g in range(PASSES):
+            nc.scalar.activation(out=w_bf[:, g], in_=w_raw[g][:].rearrange("p j m -> p m j"), func=ACT.Copy)
+
+        x_scale = keep.tile([P, S], U8, name="x_scale", align_bytes=64)
+        x_code = [keep.tile([P, S], U32, name=f"x_code{g}", align_bytes=64) for g in range(PASSES)]
+        nc.vector.tensor_copy(x_code[0][:], word_table[0][:].indirect(offsets[:]))
+        nc.vector.tensor_copy(x_scale[:], scale_table[:].indirect(offsets[:]))
+
+        w_code = keep.tile([P, PASSES * M], U32, name="w_code", align_bytes=64)
+        w_scale = keep.tile([P, PASSES * M], U8, name="w_scale", align_bytes=64)
+        nc.vector.quantize_mx(
+            out=w_code[:].bitcast(FP8X4), scales=w_scale[:], in_=w_bf[:].rearrange("p g m j -> p (g m j)")
+        )
+
+        chunks = [slice(c, c + 128) for c in range(0, S, 128)]
+        y = [psum.tile([P, cols.stop - cols.start], F32, name=f"y{c}") for c, cols in enumerate(chunks)]
+
+        def gather_words(g, cols):
+            nc.vector.tensor_copy(
+                x_code[g][:, cols], word_table[g][:].indirect(offsets[:, cols.start // 16 : cols.stop // 16])
+            )
+
+
+        def multiply(g, c):
+            nc.tensor.matmul_mx(
+                out=y[c][:],
+                lhsT=w_code[:, g * M : (g + 1) * M].bitcast(FP8X4),
+                lhsT_scale=w_scale[:, g * M : (g + 1) * M],
+                rhs=x_code[g][:, chunks[c]].bitcast(FP8X4),
+                rhs_scale=x_scale[4 * g : P, chunks[c]],
+                start=(g == 0),
+                stop=(g == PASSES - 1),
+            )
+
+
+        pos = keep.tile([P, S], F32, name="pos")
+        amp = keep.tile([P, S], F32, name="amp")
+        gain = keep.tile([P, S], F32, name="gain")
+        peak = keep.tile([P, S // D], F32, name="peak")
+        gap = keep.tile([P, S], F32, name="gap")
+        t_peak = keep.tile([P, S], F32, name="t_peak")
+        t_thr = keep.tile([P, S], F32, name="t_thr")
+        part = keep.tile([P, S], F32, name="part")
+        res = keep.tile([P, S], F32, name="res")
+
+        for c, cols in enumerate(chunks):
+            gather_words(1, cols)
+            multiply(0, c)
+            multiply(1, c)
+            nc.scalar.activation(out=pos[:, cols], in_=y[c][:], func=ACT.Relu, bias=lm_col[:], scale=1.0)
+        for c, cols in enumerate(chunks):
+            nc.scalar.activation(out=amp[:, cols], in_=y[c][:], func=ACT.Identity, bias=quarter_sc_lm[:], scale=quarter_sc[:])
+
+        spans = [slice(0, 256), slice(256, 384), slice(384, 512)]
+
+        def runs(t, cols):
+            return t[:, cols].rearrange("p (v d) -> p v d", d=D)
+
+        def st_gain(cols):
+            nc.vector.scalar_tensor_tensor(gain[:, cols], pos[:, cols], sc_col[:], pos[:, cols], ALU.mult, ALU.mult)
+            nc.scalar.activation(out=t_thr[:, cols], in_=gain[:, cols], func=ACT.Tanh, bias=-1.0, scale=2.0)
+
+        def st_peak(cols):
+            nc.vector.tensor_reduce(peak[:, cols.start // D : cols.stop // D], runs(gain, cols), AX.X, ALU.max)
+
+        def st_gap(cols):
+            n = (cols.stop - cols.start) // D
+            pk = peak[:, cols.start // D : cols.stop // D].unsqueeze(2).to_broadcast([P, n, D])
+            nc.vector.tensor_tensor(runs(gap, cols), runs(gain, cols), pk, ALU.subtract)
+            nc.scalar.activation(out=t_peak[:, cols], in_=gap[:, cols], func=ACT.Tanh, bias=0.4, scale=4.0)
+
+        def st_part(cols):
+            nc.vector.scalar_tensor_tensor(part[:, cols], t_thr[:, cols], 1.0, amp[:, cols], ALU.add, ALU.mult)
+
+        def st_res(cols):
+            nc.vector.scalar_tensor_tensor(res[:, cols], t_peak[:, cols], 1.0, part[:, cols], ALU.add, ALU.mult)
+            nc.sync.dma_start(out=out[:, cols], in_=res[:, cols])
+
+        stages = [st_gain, st_peak, st_gap, st_part, st_res]
+        LAG = 1
+        for step in range(len(stages) + LAG * (len(spans) - 1)):
+            for i, cols in reversed(list(enumerate(spans))):
+                s = step - LAG * i
+                if 0 <= s < len(stages):
+                    stages[s](cols)

@@ -35,8 +35,7 @@ def tile_picked_yspike_amp_p_kernel(tc, x_words, x_scales, w1, lm, sc, offs, out
 
         lm_col = keep.tile([P, 1], F32, name="lm_col")
         sc_col = keep.tile([P, 1], F32, name="sc_col")
-        nc.gpsimd.dma_start(out=sc_col[:], in_=sc)
-        nc.gpsimd.dma_start(out=lm_col[:], in_=lm)
+        nc.scalar.dma_start(out=sc_col[:], in_=sc)
 
         word_table = [keep.tile([P, T], U32, name=f"word_table{g}", align_bytes=64) for g in range(PASSES)]
         w_raw = [keep.tile([P, PACK, M], F32, name=f"w_raw{g}") for g in range(PASSES)]
@@ -47,36 +46,45 @@ def tile_picked_yspike_amp_p_kernel(tc, x_words, x_scales, w1, lm, sc, offs, out
                 in_=x_words[g].rearrange("p n t -> p (n t)").bitcast(I32),
             )
 
+        def load_w(g):
+            nc.sync.dma_start(out=w_raw[g][:], in_=w1[512 * g : 512 * (g + 1), :].rearrange("(p j) m -> p j m", j=PACK))
+
         load_words(0)
+        load_w(0)
         scale_rows = x_scales.bitcast(I32)
         for q in range(4):
             nc.sync.dma_start(
                 out=scale_table[32 * q : 32 * q + 4 * PASSES, :].bitcast(I32),
                 in_=scale_rows[:, 4 * q : 4 * q + 4, :],
             )
-        for g in range(PASSES):
-            nc.sync.dma_start(out=w_raw[g][:], in_=w1[512 * g : 512 * (g + 1), :].rearrange("(p j) m -> p j m", j=PACK))
+        load_w(1)
         load_words(1)
+        nc.sync.dma_start(out=lm_col[:], in_=lm)
 
         quarter_sc = keep.tile([P, 1], F32, name="quarter_sc")
         quarter_sc_lm = keep.tile([P, 1], F32, name="quarter_sc_lm")
         nc.scalar.activation(out=quarter_sc[:], in_=sc_col[:], func=ACT.Copy, scale=0.25)
-        nc.gpsimd.tensor_tensor(quarter_sc_lm[:], quarter_sc[:], lm_col[:], ALU.mult)
 
-        w_bf = keep.tile([P, PASSES, M, PACK], BF16, name="w_bf", align_bytes=64)
+        w_bf = [keep.tile([P, M, PACK], BF16, name=f"w_bf{g}", align_bytes=64) for g in range(PASSES)]
         for g in range(PASSES):
-            nc.scalar.activation(out=w_bf[:, g], in_=w_raw[g][:].rearrange("p j m -> p m j"), func=ACT.Copy)
+            nc.scalar.activation(out=w_bf[g][:], in_=w_raw[g][:].rearrange("p j m -> p m j"), func=ACT.Copy)
+        nc.scalar.activation(out=quarter_sc_lm[:], in_=lm_col[:], func=ACT.Copy, scale=quarter_sc[:])
 
         x_scale = keep.tile([P, S], U8, name="x_scale", align_bytes=64)
         x_code = [keep.tile([P, S], U32, name=f"x_code{g}", align_bytes=64) for g in range(PASSES)]
-        nc.vector.tensor_copy(x_code[0][:], word_table[0][:].indirect(offsets[:]))
-        nc.vector.tensor_copy(x_scale[:], scale_table[:].indirect(offsets[:]))
+        w_code = [keep.tile([P, M], U32, name=f"w_code{g}", align_bytes=64) for g in range(PASSES)]
+        w_scale = [keep.tile([P, M], U8, name=f"w_scale{g}", align_bytes=64) for g in range(PASSES)]
 
-        w_code = keep.tile([P, PASSES * M], U32, name="w_code", align_bytes=64)
-        w_scale = keep.tile([P, PASSES * M], U8, name="w_scale", align_bytes=64)
-        nc.vector.quantize_mx(
-            out=w_code[:].bitcast(FP8X4), scales=w_scale[:], in_=w_bf[:].rearrange("p g m j -> p (g m j)")
-        )
+        def quantise(g):
+            nc.vector.quantize_mx(
+                out=w_code[g][:].bitcast(FP8X4), scales=w_scale[g][:], in_=w_bf[g][:].rearrange("p m j -> p (m j)")
+            )
+
+        nc.vector.tensor_copy(x_code[0][:], word_table[0][:].indirect(offsets[:]))
+        quantise(0)
+        for h in range(0, S, 256):
+            nc.vector.tensor_copy(x_scale[:, h : h + 256], scale_table[:].indirect(offsets[:, h // 16 : (h + 256) // 16]))
+        quantise(1)
 
         chunks = [slice(c, c + 128) for c in range(0, S, 128)]
         y = [psum.tile([P, cols.stop - cols.start], F32, name=f"y{c}") for c, cols in enumerate(chunks)]
@@ -90,14 +98,17 @@ def tile_picked_yspike_amp_p_kernel(tc, x_words, x_scales, w1, lm, sc, offs, out
         def multiply(g, c):
             nc.tensor.matmul_mx(
                 out=y[c][:],
-                lhsT=w_code[:, g * M : (g + 1) * M].bitcast(FP8X4),
-                lhsT_scale=w_scale[:, g * M : (g + 1) * M],
+                lhsT=w_code[g][:].bitcast(FP8X4),
+                lhsT_scale=w_scale[g][:],
                 rhs=x_code[g][:, chunks[c]].bitcast(FP8X4),
                 rhs_scale=x_scale[4 * g : P, chunks[c]],
                 start=(g == 0),
                 stop=(g == PASSES - 1),
             )
 
+
+        for c in range(len(chunks)):
+            multiply(0, c)
 
         pos = keep.tile([P, S], F32, name="pos")
         amp = keep.tile([P, S], F32, name="amp")
@@ -111,7 +122,6 @@ def tile_picked_yspike_amp_p_kernel(tc, x_words, x_scales, w1, lm, sc, offs, out
 
         for c, cols in enumerate(chunks):
             gather_words(1, cols)
-            multiply(0, c)
             multiply(1, c)
             nc.scalar.activation(out=pos[:, cols], in_=y[c][:], func=ACT.Relu, bias=lm_col[:], scale=1.0)
         for c, cols in enumerate(chunks):

@@ -36,6 +36,7 @@ def tile_picked_yspike_amp_p_kernel(tc, x_words, x_scales, w1, lm, sc, offs, out
         lm_col = keep.tile([P, 1], F32, name="lm_col")
         sc_col = keep.tile([P, 1], F32, name="sc_col")
         nc.scalar.dma_start(out=sc_col[:], in_=sc)
+        nc.scalar.dma_start(out=lm_col[:], in_=lm)
 
         word_table = [keep.tile([P, T], U32, name=f"word_table{g}", align_bytes=64) for g in range(PASSES)]
         w_raw = [keep.tile([P, PACK, M], F32, name=f"w_raw{g}") for g in range(PASSES)]
@@ -59,7 +60,6 @@ def tile_picked_yspike_amp_p_kernel(tc, x_words, x_scales, w1, lm, sc, offs, out
             )
         load_w(1)
         load_words(1)
-        nc.sync.dma_start(out=lm_col[:], in_=lm)
 
         quarter_sc = keep.tile([P, 1], F32, name="quarter_sc")
         quarter_sc_lm = keep.tile([P, 1], F32, name="quarter_sc_lm")
@@ -67,7 +67,11 @@ def tile_picked_yspike_amp_p_kernel(tc, x_words, x_scales, w1, lm, sc, offs, out
 
         w_bf = [keep.tile([P, M, PACK], BF16, name=f"w_bf{g}", align_bytes=64) for g in range(PASSES)]
         for g in range(PASSES):
-            nc.scalar.activation(out=w_bf[g][:], in_=w_raw[g][:].rearrange("p j m -> p m j"), func=ACT.Copy)
+            nc.scalar.activation(
+                out=w_bf[g][:].rearrange("p (c i) j -> p c j i", i=4),
+                in_=w_raw[g][:].rearrange("p j (c i) -> p c j i", i=4),
+                func=ACT.Copy,
+            )
         nc.scalar.activation(out=quarter_sc_lm[:], in_=lm_col[:], func=ACT.Copy, scale=quarter_sc[:])
 
         x_scale = keep.tile([P, S], U8, name="x_scale", align_bytes=64)

from contextlib import ExitStack

import concourse.mybir as mybir

K, T, S, D, M = 1024, 1024, 512, 8, 128
FLOPS = 2 * K * M * S

F32 = mybir.dt.float32
BF16 = mybir.dt.bfloat16
I32 = mybir.dt.int32
U32 = mybir.dt.uint32
U16 = mybir.dt.uint16
U8 = mybir.dt.uint8
FP8X4 = mybir.dt.float8_e4m3fn_x4
ACT = mybir.ActivationFunctionType
ALU = mybir.AluOpType
AX = mybir.AxisListType

P = 128
PACK = 4
PASSES = K // (P * PACK)


def tile_picked_yspike_amp_p_kernel(tc, x_words, x_scales, w1, lm, sc, offs, out):
    nc = tc.nc
    with ExitStack() as ctx:
        keep = ctx.enter_context(tc.tile_pool(name="keep", bufs=1))
        psum = ctx.enter_context(tc.psum_pool(name="psum", bufs=1))

        offsets = keep.tile([P, S // 16], U16, name="offsets")
        nc.sync.dma_start(offsets[:], offs)

        scale_table = keep.tile([P, T], U8, name="scale_table", align_bytes=64)
        nc.vector.memset(scale_table[:].bitcast(I32), 0)

        lm_col = keep.tile([P, 1], F32, name="lm_col")
        sc_col = keep.tile([P, 1], F32, name="sc_col")
        nc.scalar.dma_start(out=sc_col[:], in_=sc)
        nc.scalar.dma_start(out=lm_col[:], in_=lm)

        word_table = [keep.tile([P, T], U32, name=f"word_table{g}", align_bytes=64) for g in range(PASSES)]
        w_raw = [keep.tile([P, PACK, M], F32, name=f"w_raw{g}") for g in range(PASSES)]

        def load_words(g):
            nc.sync.dma_start(
                out=word_table[g][:].bitcast(I32),
                in_=x_words[g].rearrange("p n t -> p (n t)").bitcast(I32),
            )

        def load_w(g):
            nc.sync.dma_start(out=w_raw[g][:], in_=w1[512 * g : 512 * (g + 1), :].rearrange("(p j) m -> p j m", j=PACK))

        load_words(0)
        load_w(0)
        scale_rows = x_scales.bitcast(I32)
        for q in range(4):
            nc.sync.dma_start(
                out=scale_table[32 * q : 32 * q + 4 * PASSES, :].bitcast(I32),
                in_=scale_rows[:, 4 * q : 4 * q + 4, :],
            )
        load_w(1)
        load_words(1)

        quarter_sc = keep.tile([P, 1], F32, name="quarter_sc")
        quarter_sc_lm = keep.tile([P, 1], F32, name="quarter_sc_lm")
        nc.scalar.activation(out=quarter_sc[:], in_=sc_col[:], func=ACT.Copy, scale=0.25)

        w_bf = [keep.tile([P, M, PACK], BF16, name=f"w_bf{g}", align_bytes=64) for g in range(PASSES)]
        for g in range(PASSES):
            nc.scalar.activation(
                out=w_bf[g][:].rearrange("p (c i) j -> p c j i", i=4),
                in_=w_raw[g][:].rearrange("p j (c i) -> p c j i", i=4),
                func=ACT.Copy,
            )
        nc.scalar.activation(out=quarter_sc_lm[:], in_=lm_col[:], func=ACT.Copy, scale=quarter_sc[:])

        x_scale = keep.tile([P, S], U8, name="x_scale", align_bytes=64)
        x_code = [keep.tile([P, S], U32, name=f"x_code{g}", align_bytes=64) for g in range(PASSES)]
        w_code = [keep.tile([P, M], U32, name=f"w_code{g}", align_bytes=64) for g in range(PASSES)]
        w_scale = [keep.tile([P, M], U8, name=f"w_scale{g}", align_bytes=64) for g in range(PASSES)]

        def quantise(g):
            nc.vector.quantize_mx(
                out=w_code[g][:].bitcast(FP8X4), scales=w_scale[g][:], in_=w_bf[g][:].rearrange("p m j -> p (m j)")
            )

        nc.vector.tensor_copy(x_code[0][:], word_table[0][:].indirect(offsets[:]))
        quantise(0)
        for h in range(0, S, 256):
            nc.vector.tensor_copy(x_scale[:, h : h + 256], scale_table[:].indirect(offsets[:, h // 16 : (h + 256) // 16]))
        quantise(1)

        chunks = [slice(c, c + 128) for c in range(0, S, 128)]
        y = [psum.tile([P, cols.stop - cols.start], F32, name=f"y{c}") for c, cols in enumerate(chunks)]

        def gather_words(g, cols):
            nc.vector.tensor_copy(
                x_code[g][:, cols], word_table[g][:].indirect(offsets[:, cols.start // 16 : cols.stop // 16])
            )


        def multiply(g, c):
            nc.tensor.matmul_mx(
                out=y[c][:],
                lhsT=w_code[g][:].bitcast(FP8X4),
                lhsT_scale=w_scale[g][:],
                rhs=x_code[g][:, chunks[c]].bitcast(FP8X4),
                rhs_scale=x_scale[4 * g : P, chunks[c]],
                start=(g == 0),
                stop=(g == PASSES - 1),
            )


        for c in range(len(chunks)):
            multiply(0, c)

        pos = keep.tile([P, S], F32, name="pos")
        amp = keep.tile([P, S], F32, name="amp")
        gain = keep.tile([P, S], F32, name="gain")
        peak = keep.tile([P, S // D], F32, name="peak")
        gap = keep.tile([P, S], F32, name="gap")
        t_peak = keep.tile([P, S], F32, name="t_peak")
        t_thr = keep.tile([P, S], F32, name="t_thr")
        part = keep.tile([P, S], F32, name="part")
        res = keep.tile([P, S], F32, name="res")

        for c, cols in enumerate(chunks):
            gather_words(1, cols)
            multiply(1, c)
            nc.scalar.activation(out=pos[:, cols], in_=y[c][:], func=ACT.Relu, bias=lm_col[:], scale=1.0)
        for c, cols in enumerate(chunks):
            nc.scalar.activation(out=amp[:, cols], in_=y[c][:], func=ACT.Identity, bias=quarter_sc_lm[:], scale=quarter_sc[:])

        spans = [slice(0, 256), slice(256, 384), slice(384, 512)]

        def runs(t, cols):
            return t[:, cols].rearrange("p (v d) -> p v d", d=D)

        def st_gain(cols):
            nc.vector.scalar_tensor_tensor(gain[:, cols], pos[:, cols], sc_col[:], pos[:, cols], ALU.mult, ALU.mult)
            nc.scalar.activation(out=t_thr[:, cols], in_=gain[:, cols], func=ACT.Tanh, bias=-1.0, scale=2.0)

        def st_peak(cols):
            nc.vector.tensor_reduce(peak[:, cols.start // D : cols.stop // D], runs(gain, cols), AX.X, ALU.max)

        def st_gap(cols):
            n = (cols.stop - cols.start) // D
            pk = peak[:, cols.start // D : cols.stop // D].unsqueeze(2).to_broadcast([P, n, D])
            nc.vector.tensor_tensor(runs(gap, cols), runs(gain, cols), pk, ALU.subtract)
            nc.scalar.activation(out=t_peak[:, cols], in_=gap[:, cols], func=ACT.Tanh, bias=0.4, scale=4.0)

        def st_part(cols):
            nc.vector.scalar_tensor_tensor(part[:, cols], t_thr[:, cols], 1.0, amp[:, cols], ALU.add, ALU.mult)

        def st_res(cols):
            nc.vector.scalar_tensor_tensor(res[:, cols], t_peak[:, cols], 1.0, part[:, cols], ALU.add, ALU.mult)
            nc.sync.dma_start(out=out[:, cols], in_=res[:, cols])

        stages = [st_gain, st_peak, st_gap, st_part, st_res]
        LAG = 1
        for step in range(len(stages) + LAG * (len(spans) - 1)):
            for i, cols in reversed(list(enumerate(spans))):
                s = step - LAG * i
                if 0 <= s < len(stages):
                    stages[s](cols)
